import numpy as np
import ml_dtypes


def mxq(x, axis, fmt="e4m3"):
    dtype, down = {"e4m3": (ml_dtypes.float8_e4m3fn, 7), "e5m2": (ml_dtypes.float8_e5m2, 14)}[fmt]
    v = np.moveaxis(np.asarray(x, np.float32).astype(ml_dtypes.bfloat16).astype(np.float64), axis, -1)
    blocks = v.reshape(v.shape[:-1] + (-1, 32))
    amax = np.abs(blocks).max(-1, keepdims=True)
    byte = np.maximum(np.where(amax > 0, np.frexp(amax)[1] - 1 + 127, 0) - down, 1)
    scale = np.exp2(byte - 127.0)
    codes = (blocks / scale).astype(np.float32).astype(dtype).astype(np.float64)
    return np.moveaxis((codes * scale).reshape(v.shape), -1, axis)


WIDE = False


def mx_kscale(k):
    if not WIDE:
        return np.ones(k)
    levels = np.array([10, -10, 5, -5, 0])
    if k % 512:
        return np.exp2(np.random.permutation(np.resize(levels, k // 32))).repeat(32)
    a = np.empty((k // 512, 16))
    for p in range(k // 512):
        a[p, :8] = np.random.permutation(np.resize(levels, 8))
        for g in range(8):
            far = levels[np.abs(levels - a[p, g]) >= 10]
            a[p, g + 8] = far[np.random.randint(len(far))]
    return np.exp2(a.ravel()).repeat(32)


def f64(x):
    return np.asarray(x).astype(np.float64)


def striped(idx):
    return np.tile(idx.reshape(-1, 16).T, (8, 1)).astype(np.uint16)


def unstriped(offs):
    return offs[:16].T.reshape(-1).astype(np.int64)


E2M1 = np.array([0.0, 0.5, 1.0, 1.5, 2.0, 3.0, 4.0, 6.0, -0.0, -0.5, -1.0, -1.5, -2.0, -3.0, -4.0, -6.0])


def pack_weight(w, fmt):
    k, n = w.shape
    w = f64(np.asarray(w, np.float32).astype(ml_dtypes.bfloat16)).reshape(k // 32, 32, n)
    amax = np.abs(w).max(1)
    if fmt == "e4m3":
        byte = np.frexp(amax)[1] - 1 + 127 - 7
    else:
        mant, ex = np.frexp(amax / 6.0)
        byte = np.where(mant > 0.5, ex, ex - 1) + 127
    byte = np.clip(np.where(amax > 0, byte, 1), 1, 254)
    scaled = (w * np.exp2(127.0 - byte)[:, None, :]).reshape(k, n).astype(np.float32)
    by_word = np.ascontiguousarray(scaled.reshape(k // 512, 128, 4, n).transpose(0, 1, 3, 2))
    if fmt == "e4m3":
        words = by_word.astype(ml_dtypes.float8_e4m3fn).view(np.uint8)
    else:
        c = by_word.astype(ml_dtypes.float4_e2m1fn).view(np.uint8) & 0xF
        words = (c[..., 0::2] | (c[..., 1::2] << 4)).reshape(k // 512, 128, 2 * n)
    return np.ascontiguousarray(words), np.ascontiguousarray(byte.astype(np.uint8).reshape(k // 512, 16, n))


def unpack_weight(words, scales, fmt):
    g, _, n = scales.shape
    words = np.ascontiguousarray(words).reshape(g, 128, n, -1)
    if fmt == "e4m3":
        vals = words.view(ml_dtypes.float8_e4m3fn).astype(np.float64)
    else:
        nib = np.empty((g, 128, n, 4), np.uint8)
        nib[..., 0::2] = words & 0xF
        nib[..., 1::2] = words >> 4
        vals = E2M1[nib]
    vals = vals * np.repeat(np.exp2(scales.astype(np.float64) - 127.0), 8, axis=1)[..., None]
    return vals.transpose(0, 1, 3, 2).reshape(g * 512, n)


def gelu(v):
    return 0.5 * v * (1.0 + np.tanh(np.sqrt(2.0 / np.pi) * (v + 0.044715 * v**3)))


K, H, M, N, T, S, T2, P = 512, 1024, 1024, 384, 2048, 1024, 2048, 1024


def setup_inputs():
    n = np.random.standard_normal
    s = mx_kscale(K)[:, None]
    u = mx_kscale(H)[:, None]
    u2 = mx_kscale(M)[:, None]
    tab_words, tab_scales = pack_weight(n((K, T)) * s, "e4m3")
    w2_words, w2_scales = pack_weight(n((H, M)) / np.sqrt(H) / u, "e2m1")
    return {
        "tab_words": tab_words,
        "tab_scales": tab_scales,
        "offs": striped(np.random.permutation(T)[:S]),
        "offs2": striped(np.random.permutation(T2)[:S]),
        "offs3": striped(np.random.permutation(T2)[:P]),
        "offs4": striped(np.random.permutation(T2)[:P]),
        "w1": (1.4 * n((K, H)) / np.sqrt(K) / s).astype(np.float32),
        "gain": (1.3 * np.exp(0.3 * n(H)) * u[:, 0]).astype(np.float32),
        "wgs": np.exp(0.3 * n((128, S))).astype(np.float32),
        "page0": (n((H, T2)) * u).astype(np.float32),
        "level": (0.8 * n((H, P)) * u).astype(np.float32),
        "w2_words": w2_words,
        "w2_scales": w2_scales,
        "mgain": (np.exp(0.3 * n(M)) * u2[:, 0]).astype(np.float32),
        "w3": (n((M, N)) / np.sqrt(M) / u2).astype(np.float32),
    }


def reference(tab_words, tab_scales, offs, offs2, offs3, offs4, w1, gain, wgs, page0, level, w2_words, w2_scales, mgain, w3):
    v = unpack_weight(tab_words, tab_scales, "e4m3")[:, unstriped(offs)]
    h = f64(gain)[:, None] * np.tanh(mxq(f64(w1), 0, "e4m3").T @ v)
    before = f64(page0)
    page = before.copy()
    page[:, unstriped(offs2)] = np.tile(f64(wgs), (H // 128, 1)) * h
    x = np.maximum(page[:, unstriped(offs3)], before[:, unstriped(offs4)]) - f64(level)
    xq = mxq(x, 0, "e4m3")
    y = unpack_weight(w2_words, w2_scales, "e2m1").T @ xq
    d = 0.5 * y * (1.0 + np.tanh(np.sqrt(2.0 / np.pi) * (y + 0.044715 * y ** 3)))
    dq = mxq(f64(mgain)[:, None] * d, 0, "e4m3")
    return mxq(f64(w3), 0, "e4m3").T @ dq

@@ -1,0 +1,276 @@
+from contextlib import ExitStack
+
+import concourse.mybir as mybir
+
+K, H, M, N, T, S, T2, PJ = 512, 1024, 1024, 384, 2048, 1024, 2048, 1024
+FLOPS = 2 * (K * H * S + H * M * PJ + M * N * PJ)
+
+F32 = mybir.dt.float32
+BF16 = mybir.dt.bfloat16
+I32 = mybir.dt.int32
+U32 = mybir.dt.uint32
+U16 = mybir.dt.uint16
+U8 = mybir.dt.uint8
+FP8X4 = mybir.dt.float8_e4m3fn_x4
+FP4X4 = mybir.dt.float4_e2m1fn_x4
+ALU = mybir.AluOpType
+ACT = mybir.ActivationFunctionType
+
+P = 128
+BANK = 512
+CHUNKS = [256, 256, 256, 128, 128]
+
+
+def tile_list_pool_breeding_scores_kernel(
+    tc, tab_words, tab_scales, offs, offs2, offs3, offs4, w1, gain, wgs, page0, level, w2_words, w2_scales, mgain, w3, out
+):
+    nc = tc.nc
+    with ExitStack() as ctx:
+        keep = ctx.enter_context(tc.tile_pool(name="keep", bufs=1))
+        psum = ctx.enter_context(tc.psum_pool(name="psum", bufs=1))
+
+        list1 = keep.tile([P, S // 16], U16, name="list1")
+        list2 = keep.tile([P, S // 16], U16, name="list2")
+        list3 = keep.tile([P, PJ // 16], U16, name="list3")
+        list4 = keep.tile([P, PJ // 16], U16, name="list4")
+        pages = [keep.tile([P, T2], F32, name=f"page{s}") for s in range(8)]
+        levels = [keep.tile([P, PJ], F32, name=f"level{s}") for s in range(8)]
+        olds = [keep.tile([P, 4, PJ], F32, name=f"old{a}") for a in range(2)]
+        gain_sb = keep.tile([P, 2, 4], F32, name="gain_sb")
+        mgain_sb = keep.tile([P, 2, 4], F32, name="mgain_sb")
+        w2_codes = keep.tile([P, 2, 2 * M], U8, name="w2_codes", align_bytes=64)
+        w2_planes = keep.tile([P, 2, M], U8, name="w2_planes", align_bytes=64)
+        w3_codes = [keep.tile([P, N], U32, name=f"w3_codes{b}", align_bytes=64) for b in range(2)]
+        w3_planes = [keep.tile([P, N], U8, name=f"w3_planes{b}", align_bytes=64) for b in range(2)]
+
+        page_rows = page0.rearrange("(a p t) c -> a t p c", a=2, t=4)
+        level_rows = level.rearrange("(a p t) c -> a t p c", a=2, t=4)
+        wgs_rows = wgs.rearrange("(p t) j -> p t j", t=4)
+
+        with tc.tile_pool(name="head", bufs=1) as head:
+            tab_sb = head.tile([P, T], I32, name="tab_sb")
+            tab_plane = head.tile([P, T], U8, name="tab_plane")
+            v_codes = head.tile([P, S], U32, name="v_codes", align_bytes=64)
+            v_plane = head.tile([P, S], U8, name="v_plane", align_bytes=64)
+            wgs_first = head.tile([P, S], F32, name="wgs_first")
+            wgs_rest = head.tile([P, 3, S], F32, name="wgs_rest")
+            w2_raw = head.tile([P, 2, 2 * M], U8, name="w2_raw")
+            w2_raw_planes = head.tile([P, 2, M], U8, name="w2_raw_planes")
+            w1_codes = [head.tile([P, 512], U32, name=f"w1_codes{a}", align_bytes=64) for a in range(2)]
+            w1_planes = [head.tile([P, 512], U8, name=f"w1_planes{a}", align_bytes=64) for a in range(2)]
+
+            def load_page(s):
+                nc.sync.dma_start(out=pages[s][:], in_=page_rows[s // 4, s % 4])
+                nc.sync.dma_start(out=levels[s][:], in_=level_rows[s // 4, s % 4])
+
+            def load_w1(a):
+                raw = head.tile([P, 4, 512], F32, name="w1_raw", tag="raw", bufs=2)
+                nc.sync.dma_start(out=raw[:], in_=w1[:, 512 * a : 512 * (a + 1)].rearrange("(p j) c -> p j c", j=4))
+                return raw
+
+            def quantize_w1(a, raw):
+                grouped = head.tile([P, 2048], BF16, name="w1_grouped", tag="grouped", bufs=2, align_bytes=64)
+                nc.scalar.copy(
+                    out=grouped[:].rearrange("p (t m j) -> p m t j", t=4, j=4),
+                    in_=raw[:].rearrange("p j (m t) -> p m t j", t=4),
+                )
+                nc.vector.quantize_mx(out=w1_codes[a][:].bitcast(FP8X4), scales=w1_planes[a][:], in_=grouped[:])
+
+            def load_w3(b):
+                raw = head.tile([P, 4, N], F32, name="w3_raw", tag="raw", bufs=2)
+                nc.sync.dma_start(out=raw[:], in_=w3[512 * b : 512 * (b + 1), :].rearrange("(p t) n -> p t n", t=4))
+                return raw
+
+            def quantize_w3(b, raw):
+                grouped = head.tile([P, 4 * N], BF16, name="w3_grouped", tag="grouped", bufs=2, align_bytes=64)
+                nc.scalar.copy(
+                    out=grouped[:].rearrange("p (c i t) -> p c t i", t=4, i=4),
+                    in_=raw[:].rearrange("p t (c i) -> p c t i", i=4),
+                )
+                nc.vector.quantize_mx(out=w3_codes[b][:].bitcast(FP8X4), scales=w3_planes[b][:], in_=grouped[:])
+
+            def make_h(s):
+                a, t = divmod(s, 4)
+                h = head.tile([P, S], F32, name="h", tag="h", bufs=3)
+                for half in range(2):
+                    cols = slice(BANK * half, BANK * (half + 1))
+                    acc = psum.tile([P, BANK], F32, name="acc1", tag="wide", bufs=5)
+                    nc.tensor.matmul_mx(
+                        out=acc[:],
+                        lhsT=w1_codes[a][:, P * t : P * (t + 1)].bitcast(FP8X4),
+                        lhsT_scale=w1_planes[a][:, P * t : P * (t + 1)],
+                        rhs=v_codes[:, cols].bitcast(FP8X4),
+                        rhs_scale=v_plane[:, cols],
+                        start=True,
+                        stop=True,
+                    )
+                    nc.scalar.activation(out=h[:, cols], in_=acc[:], func=ACT.Tanh)
+                    nc.scalar.activation(out=h[:, cols], in_=h[:, cols], func=ACT.Copy, scale=gain_sb[:, a, t : t + 1])
+                return h
+
+            def rewrite_page(s, h):
+                a, t = divmod(s, 4)
+                nc.vector.tensor_tensor(olds[a][:, t, :], pages[s][:].indirect(list4[:]), levels[s][:], ALU.subtract)
+                weights = wgs_first[:] if t == 0 else wgs_rest[:, t - 1, :]
+                nc.vector.tensor_tensor(pages[s][:].indirect(list2[:]), h[:], weights, ALU.mult)
+
+            nc.vector.memset(tab_plane[:].bitcast(I32), 0)
+            nc.gpsimd.memset(w2_raw_planes[:].rearrange("p a c -> p (a c)").bitcast(I32), 0)
+
+            nc.sync.dma_start(list1[:], offs)
+            for q in range(4):
+                nc.sync.dma_start(
+                    out=tab_plane[32 * q : 32 * q + 4, :].bitcast(I32), in_=tab_scales[0, 4 * q : 4 * q + 4, :].bitcast(I32)
+                )
+            nc.sync.dma_start(out=tab_sb[:], in_=tab_words[0].rearrange("p n i -> p (n i)").bitcast(I32))
+            w1_raw0 = load_w1(0)
+            load_page(0)
+            nc.sync.dma_start(list4[:], offs4)
+            nc.sync.dma_start(list2[:], offs2)
+            nc.sync.dma_start(out=gain_sb[:], in_=gain.rearrange("(a p t) -> p a t", a=2, t=4))
+            for q in range(4):
+                nc.sync.dma_start(out=wgs_first[32 * q : 32 * (q + 1), :], in_=wgs_rows[:, 0, :])
+            load_page(1)
+            for q in range(4):
+                nc.sync.dma_start(out=wgs_rest[32 * q : 32 * (q + 1), :, :], in_=wgs_rows[:, 1:4, :])
+            load_page(2)
+            w1_raw1 = load_w1(1)
+            load_page(3)
+            load_page(4)
+            for a in range(2):
+                nc.sync.dma_start(out=w2_raw[:, a, :].bitcast(I32), in_=w2_words[a].bitcast(I32))
+            for q in range(4):
+                nc.sync.dma_start(
+                    out=w2_raw_planes[32 * q : 32 * q + 4, :, :].bitcast(I32),
+                    in_=w2_scales[:, 4 * q : 4 * q + 4, :].rearrange("a r c -> r a c").bitcast(I32),
+                )
+            load_page(5)
+            load_page(6)
+            load_page(7)
+            nc.sync.dma_start(list3[:], offs3)
+            nc.sync.dma_start(out=mgain_sb[:], in_=mgain.rearrange("(b p t) -> p b t", b=2, t=4))
+
+            nc.vector.tensor_copy(v_plane[:], tab_plane[:].indirect(list1[:]))
+            nc.vector.tensor_copy(v_codes[:], tab_sb[:].bitcast(U32).indirect(list1[:]))
+            quantize_w1(0, w1_raw0)
+            for s in range(8):
+                if s == 2:
+                    quantize_w1(1, w1_raw1)
+                if s == 4:
+                    nc.vector.tensor_copy(
+                        out=w2_codes[:].bitcast(U16).rearrange("p a (b t q) -> p (a b) t q", b=2, t=4),
+                        in_=w2_raw[:].bitcast(U16).rearrange("p a (b q t) -> p (a b) t q", b=2, t=4),
+                    )
+                    nc.vector.tensor_copy(
+                        out=w2_planes[:].rearrange("p a (b t q) -> p (a b) t q", b=2, t=4),
+                        in_=w2_raw_planes[:].rearrange("p a (b q t) -> p (a b) t q", b=2, t=4),
+                    )
+                if s in (5, 6):
+                    quantize_w3(s - 5, load_w3(s - 5))
+                rewrite_page(s, make_h(s))
+
+        tail = ctx.enter_context(tc.tile_pool(name="tail", bufs=1))
+        out_rows = out.rearrange("(u p) j -> p u j", p=P)
+
+        def make_x(j0, n):
+            codes = tail.tile([P, 2, n], U32, name="x_codes", bufs=2, align_bytes=64)
+            plane = tail.tile([P, 2, n], U8, name="x_plane", bufs=2, align_bytes=64)
+            grouped = tail.tile([P, 2, 4 * n], BF16, name="x_grouped", bufs=2, align_bytes=64)
+            news = []
+            for a in range(2):
+                new = tail.tile([P, 4, n], F32, name="new", bufs=3)
+                for t in range(4):
+                    s = 4 * a + t
+                    nc.vector.tensor_tensor(
+                        new[:, t, :],
+                        pages[s][:].indirect(list3[:, j0 // 16 : (j0 + n) // 16]),
+                        levels[s][:, j0 : j0 + n],
+                        ALU.subtract,
+                    )
+                news.append(new)
+            for a in range(2):
+                nc.vector.tensor_tensor(
+                    grouped[:, a, :].rearrange("p (c i t) -> p c t i", t=4, i=4),
+                    news[a][:].rearrange("p t (c i) -> p c t i", i=4),
+                    olds[a][:, :, j0 : j0 + n].rearrange("p t (c i) -> p c t i", i=4),
+                    ALU.max,
+                )
+            for a in range(2):
+                nc.vector.quantize_mx(out=codes[:, a, :].bitcast(FP8X4), scales=plane[:, a, :], in_=grouped[:, a, :])
+            return codes, plane
+
+        def make_d(n, codes, plane, on_vector):
+            per_bank = BANK // n
+            groups = []
+            for b in range(2):
+                act = tail.tile([P, 4, n], F32, name="act", bufs=2)
+                for t0 in range(0, 4, per_bank):
+                    acc = psum.tile([P, per_bank, n], F32, name="acc2", tag="wide", bufs=5)
+                    for u in range(per_bank):
+                        c0 = 512 * b + P * (t0 + u)
+                        for a in range(2):
+                            nc.tensor.matmul_mx(
+                                out=acc[:, u, :],
+                                lhsT=w2_codes[:, a, 2 * c0 : 2 * (c0 + P)].bitcast(FP4X4),
+                                lhsT_scale=w2_planes[:, a, c0 : c0 + P],
+                                rhs=codes[:, a, :].bitcast(FP8X4),
+                                rhs_scale=plane[:, a, :],
+                                start=(a == 0),
+                                stop=(a == 1),
+                            )
+                    nc.scalar.activation(out=act[:, t0 : t0 + per_bank, :], in_=acc[:], func=ACT.Gelu_apprx_tanh)
+                grouped = tail.tile([P, 4 * n], BF16, name="d_grouped", bufs=3, align_bytes=64)
+                if on_vector:
+                    nc.vector.tensor_tensor(
+                        grouped[:].rearrange("p (c i t) -> p c t i", t=4, i=4),
+                        act[:].rearrange("p t (c i) -> p c t i", i=4),
+                        mgain_sb[:, b, :].unsqueeze(1).unsqueeze(3).to_broadcast([P, n // 4, 4, 4]),
+                        ALU.mult,
+                    )
+                else:
+                    scaled = tail.tile([P, 4, n], BF16, name="scaled", bufs=2)
+                    for t in range(4):
+                        nc.scalar.activation(
+                            out=scaled[:, t, :], in_=act[:, t, :], func=ACT.Copy, scale=mgain_sb[:, b, t : t + 1]
+                        )
+                    nc.scalar.copy(
+                        out=grouped[:].rearrange("p (c i t) -> p c t i", t=4, i=8),
+                        in_=scaled[:].rearrange("p t (c i) -> p c t i", i=8),
+                    )
+                groups.append(grouped)
+            return groups
+
+        def finish(j0, n, groups):
+            codes = tail.tile([P, 2, n], U32, name="d_codes", bufs=2, align_bytes=64)
+            plane = tail.tile([P, 2, n], U8, name="d_plane", bufs=2, align_bytes=64)
+            for b in range(2):
+                nc.vector.quantize_mx(out=codes[:, b, :].bitcast(FP8X4), scales=plane[:, b, :], in_=groups[b][:])
+            result = tail.tile([P, 3, n], F32, name="result", bufs=2)
+            per_bank = BANK // n
+            for u0 in range(0, 3, per_bank):
+                count = min(per_bank, 3 - u0)
+                acc = psum.tile([P, count, n], F32, name="acc3", tag="scores", bufs=3)
+                for u in range(count):
+                    c0 = P * (u0 + u)
+                    for b in range(2):
+                        nc.tensor.matmul_mx(
+                            out=acc[:, u, :],
+                            lhsT=w3_codes[b][:, c0 : c0 + P].bitcast(FP8X4),
+                            lhsT_scale=w3_planes[b][:, c0 : c0 + P],
+                            rhs=codes[:, b, :].bitcast(FP8X4),
+                            rhs_scale=plane[:, b, :],
+                            start=(b == 0),
+                            stop=(b == 1),
+                        )
+                nc.scalar.copy(out=result[:, u0 : u0 + count, :], in_=acc[:])
+            nc.sync.dma_start(out=out_rows[:, :, j0 : j0 + n], in_=result[:])
+
+        starts = [sum(CHUNKS[:c]) for c in range(len(CHUNKS))]
+        pending = None
+        for c, n in enumerate(CHUNKS):
+            codes, plane = make_x(starts[c], n)
+            if pending is not None:
+                finish(*pending)
+            groups = make_d(n, codes, plane, c == len(CHUNKS) - 1)
+            pending = (starts[c], n, groups)
+        finish(*pending)

@@ -18,7 +18,8 @@ ACT = mybir.ActivationFunctionType
 
 P = 128
 BANK = 512
-CHUNKS = [256, 256, 256, 128, 128]
+GROUP = 256
+FIRST_PIECES = [(0, 256), (256, 512), (512, 1024)]
 
 
 def tile_list_pool_breeding_scores_kernel(
@@ -34,10 +35,11 @@ def tile_list_pool_breeding_scores_kernel(
         list3 = keep.tile([P, PJ // 16], U16, name="list3")
         list4 = keep.tile([P, PJ // 16], U16, name="list4")
         pages = [keep.tile([P, T2], F32, name=f"page{s}") for s in range(8)]
+        untouched = [keep.tile([P, T2], F32, name=f"untouched{t}") for t in range(4)]
         levels = [keep.tile([P, PJ], F32, name=f"level{s}") for s in range(8)]
-        olds = [keep.tile([P, 4, PJ], F32, name=f"old{a}") for a in range(2)]
+        old_upper = keep.tile([P, 4, PJ], F32, name="old_upper")
         gain_sb = keep.tile([P, 2, 4], F32, name="gain_sb")
-        mgain_sb = keep.tile([P, 2, 4], F32, name="mgain_sb")
+        mgain_sb = [keep.tile([P, 4], F32, name=f"mgain_sb{b}") for b in range(2)]
         w2_codes = keep.tile([P, 2, 2 * M], U8, name="w2_codes", align_bytes=64)
         w2_planes = keep.tile([P, 2, M], U8, name="w2_planes", align_bytes=64)
         w3_codes = [keep.tile([P, N], U32, name=f"w3_codes{b}", align_bytes=64) for b in range(2)]
@@ -46,6 +48,8 @@ def tile_list_pool_breeding_scores_kernel(
         page_rows = page0.rearrange("(a p t) c -> a t p c", a=2, t=4)
         level_rows = level.rearrange("(a p t) c -> a t p c", a=2, t=4)
         wgs_rows = wgs.rearrange("(p t) j -> p t j", t=4)
+        w3_rows = w3.rearrange("(b g t i) n -> b i g t n", b=2, t=4, i=8)
+        mgain_rows = mgain.rearrange("(b g t i) -> b i g t", b=2, t=4, i=8)
 
         with tc.tile_pool(name="head", bufs=1) as head:
             tab_sb = head.tile([P, T], I32, name="tab_sb")
@@ -53,36 +57,37 @@ def tile_list_pool_breeding_scores_kernel(
             v_codes = head.tile([P, S], U32, name="v_codes", align_bytes=64)
             v_plane = head.tile([P, S], U8, name="v_plane", align_bytes=64)
             wgs_first = head.tile([P, S], F32, name="wgs_first")
-            wgs_rest = head.tile([P, 3, S], F32, name="wgs_rest")
+            wgs_second = head.tile([P, S], F32, name="wgs_second")
+            wgs_rest = head.tile([P, 2, S], F32, name="wgs_rest")
             w2_raw = head.tile([P, 2, 2 * M], U8, name="w2_raw")
             w2_raw_planes = head.tile([P, 2, M], U8, name="w2_raw_planes")
             w1_codes = [head.tile([P, 512], U32, name=f"w1_codes{a}", align_bytes=64) for a in range(2)]
             w1_planes = [head.tile([P, 512], U8, name=f"w1_planes{a}", align_bytes=64) for a in range(2)]
-
-            def load_page(s):
-                nc.sync.dma_start(out=pages[s][:], in_=page_rows[s // 4, s % 4])
-                nc.sync.dma_start(out=levels[s][:], in_=level_rows[s // 4, s % 4])
 
             def load_w1(a):
                 raw = head.tile([P, 4, 512], F32, name="w1_raw", tag="raw", bufs=2)
                 nc.sync.dma_start(out=raw[:], in_=w1[:, 512 * a : 512 * (a + 1)].rearrange("(p j) c -> p j c", j=4))
                 return raw
 
-            def quantize_w1(a, raw):
-                grouped = head.tile([P, 2048], BF16, name="w1_grouped", tag="grouped", bufs=2, align_bytes=64)
+            def quantize_w1(a, raw, t0, t1):
+                grouped = head.tile([P, (t1 - t0) * 512], BF16, name=f"w1_grouped{t1 - t0}", align_bytes=64)
                 nc.scalar.copy(
-                    out=grouped[:].rearrange("p (t m j) -> p m t j", t=4, j=4),
-                    in_=raw[:].rearrange("p j (m t) -> p m t j", t=4),
+                    out=grouped[:].rearrange("p (t m j) -> p m t j", m=P, j=4),
+                    in_=raw[:].rearrange("p j (m t) -> p m t j", t=4)[:, :, t0:t1, :],
                 )
-                nc.vector.quantize_mx(out=w1_codes[a][:].bitcast(FP8X4), scales=w1_planes[a][:], in_=grouped[:])
+                cols = slice(P * t0, P * t1)
+                nc.vector.quantize_mx(out=w1_codes[a][:, cols].bitcast(FP8X4), scales=w1_planes[a][:, cols], in_=grouped[:])
 
             def load_w3(b):
                 raw = head.tile([P, 4, N], F32, name="w3_raw", tag="raw", bufs=2)
-                nc.sync.dma_start(out=raw[:], in_=w3[512 * b : 512 * (b + 1), :].rearrange("(p t) n -> p t n", t=4))
+                for i in range(8):
+                    nc.sync.dma_start(out=raw[i:P:8, :, :], in_=w3_rows[b, i])
+                    with nc.allow_non_contiguous_dma(reason="one gain to a partition and slot"):
+                        nc.sync.dma_start(out=mgain_sb[b][i:P:8, :], in_=mgain_rows[b, i])
                 return raw
 
             def quantize_w3(b, raw):
-                grouped = head.tile([P, 4 * N], BF16, name="w3_grouped", tag="grouped", bufs=2, align_bytes=64)
+                grouped = head.tile([P, 4 * N], BF16, name="w3_grouped", bufs=2, align_bytes=64)
                 nc.scalar.copy(
                     out=grouped[:].rearrange("p (c i t) -> p c t i", t=4, i=4),
                     in_=raw[:].rearrange("p t (c i) -> p c t i", i=4),
@@ -92,9 +97,9 @@ def tile_list_pool_breeding_scores_kernel(
             def make_h(s):
                 a, t = divmod(s, 4)
                 h = head.tile([P, S], F32, name="h", tag="h", bufs=3)
-                for half in range(2):
-                    cols = slice(BANK * half, BANK * (half + 1))
-                    acc = psum.tile([P, BANK], F32, name="acc1", tag="wide", bufs=5)
+                for j0, j1 in (FIRST_PIECES if s == 0 else [(0, BANK), (BANK, S)]):
+                    cols = slice(j0, j1)
+                    acc = psum.tile([P, j1 - j0], F32, name="acc1")
                     nc.tensor.matmul_mx(
                         out=acc[:],
                         lhsT=w1_codes[a][:, P * t : P * (t + 1)].bitcast(FP8X4),
@@ -110,33 +115,44 @@ def tile_list_pool_breeding_scores_kernel(
 
             def rewrite_page(s, h):
                 a, t = divmod(s, 4)
-                nc.vector.tensor_tensor(olds[a][:, t, :], pages[s][:].indirect(list4[:]), levels[s][:], ALU.subtract)
-                weights = wgs_first[:] if t == 0 else wgs_rest[:, t - 1, :]
-                nc.vector.tensor_tensor(pages[s][:].indirect(list2[:]), h[:], weights, ALU.mult)
+                if a == 1:
+                    nc.vector.tensor_tensor(old_upper[:, t, :], pages[s][:].indirect(list4[:]), levels[s][:], ALU.subtract)
+                weights = [wgs_first[:], wgs_second[:], wgs_rest[:, 0, :], wgs_rest[:, 1, :]][t]
+                for j0, j1 in (FIRST_PIECES if s == 0 else [(0, S)]):
+                    nc.vector.tensor_tensor(
+                        pages[s][:].indirect(list2[:, j0 // 16 : j1 // 16]), h[:, j0:j1], weights[:, j0:j1], ALU.mult
+                    )
 
             nc.vector.memset(tab_plane[:].bitcast(I32), 0)
-            nc.gpsimd.memset(w2_raw_planes[:].rearrange("p a c -> p (a c)").bitcast(I32), 0)
 
             nc.sync.dma_start(list1[:], offs)
+            nc.sync.dma_start(out=gain_sb[:], in_=gain.rearrange("(a p t) -> p a t", a=2, t=4))
+            warm = head.tile([P, 1], F32, name="warm")
+            nc.gpsimd.memset(warm[:], 0.0)
+            nc.scalar.activation(out=warm[:], in_=warm[:], func=ACT.Tanh)
+            nc.sync.dma_start(out=tab_sb[:], in_=tab_words[0].rearrange("p n i -> p (n i)").bitcast(I32))
+            nc.gpsimd.memset(w2_raw_planes[:].rearrange("p a c -> p (a c)").bitcast(I32), 0)
             for q in range(4):
                 nc.sync.dma_start(
                     out=tab_plane[32 * q : 32 * q + 4, :].bitcast(I32), in_=tab_scales[0, 4 * q : 4 * q + 4, :].bitcast(I32)
                 )
-            nc.sync.dma_start(out=tab_sb[:], in_=tab_words[0].rearrange("p n i -> p (n i)").bitcast(I32))
             w1_raw0 = load_w1(0)
-            load_page(0)
-            nc.sync.dma_start(list4[:], offs4)
+            nc.sync.dma_start(out=pages[0][:], in_=page_rows[0, 0])
             nc.sync.dma_start(list2[:], offs2)
-            nc.sync.dma_start(out=gain_sb[:], in_=gain.rearrange("(a p t) -> p a t", a=2, t=4))
-            for q in range(4):
+            for q in (0, 2, 1, 3):
                 nc.sync.dma_start(out=wgs_first[32 * q : 32 * (q + 1), :], in_=wgs_rows[:, 0, :])
-            load_page(1)
-            for q in range(4):
-                nc.sync.dma_start(out=wgs_rest[32 * q : 32 * (q + 1), :, :], in_=wgs_rows[:, 1:4, :])
-            load_page(2)
+            nc.sync.dma_start(out=pages[1][:], in_=page_rows[0, 1])
+            for q in (0, 2, 1, 3):
+                nc.sync.dma_start(out=wgs_second[32 * q : 32 * (q + 1), :], in_=wgs_rows[:, 1, :])
+            nc.sync.dma_start(out=pages[2][:], in_=page_rows[0, 2])
+            for q in (0, 2, 1, 3):
+                nc.sync.dma_start(out=wgs_rest[32 * q : 32 * (q + 1), :, :], in_=wgs_rows[:, 2:4, :])
             w1_raw1 = load_w1(1)
-            load_page(3)
-            load_page(4)
+            nc.sync.dma_start(out=pages[3][:], in_=page_rows[0, 3])
+            nc.sync.dma_start(list4[:], offs4)
+            for s in range(4, 8):
+                nc.sync.dma_start(out=pages[s][:], in_=page_rows[1, s - 4])
+                nc.sync.dma_start(out=levels[s][:], in_=level_rows[1, s - 4])
             for a in range(2):
                 nc.sync.dma_start(out=w2_raw[:, a, :].bitcast(I32), in_=w2_words[a].bitcast(I32))
             for q in range(4):
@@ -144,133 +160,167 @@ def tile_list_pool_breeding_scores_kernel(
                     out=w2_raw_planes[32 * q : 32 * q + 4, :, :].bitcast(I32),
                     in_=w2_scales[:, 4 * q : 4 * q + 4, :].rearrange("a r c -> r a c").bitcast(I32),
                 )
-            load_page(5)
-            load_page(6)
-            load_page(7)
+            w3_raws = [load_w3(b) for b in range(2)]
             nc.sync.dma_start(list3[:], offs3)
-            nc.sync.dma_start(out=mgain_sb[:], in_=mgain.rearrange("(b p t) -> p b t", b=2, t=4))
+            for t in range(4):
+                nc.sync.dma_start(out=untouched[t][:], in_=page_rows[0, t])
+                nc.sync.dma_start(out=levels[t][:], in_=level_rows[0, t])
 
-            nc.vector.tensor_copy(v_plane[:], tab_plane[:].indirect(list1[:]))
             nc.vector.tensor_copy(v_codes[:], tab_sb[:].bitcast(U32).indirect(list1[:]))
-            quantize_w1(0, w1_raw0)
+            nc.vector.tensor_copy(v_plane[:], tab_plane[:].indirect(list1[:]))
+            quantize_w1(0, w1_raw0, 0, 1)
+            quantize_w1(0, w1_raw0, 1, 4)
             for s in range(8):
                 if s == 2:
-                    quantize_w1(1, w1_raw1)
-                if s == 4:
+                    quantize_w1(1, w1_raw1, 0, 4)
+                if s == 6:
                     nc.vector.tensor_copy(
-                        out=w2_codes[:].bitcast(U16).rearrange("p a (b t q) -> p (a b) t q", b=2, t=4),
-                        in_=w2_raw[:].bitcast(U16).rearrange("p a (b q t) -> p (a b) t q", b=2, t=4),
+                        out=w2_codes[:].bitcast(I32).rearrange("p a (b t g w) -> p (a b) t g w", b=2, t=4, w=4),
+                        in_=w2_raw[:].bitcast(I32).rearrange("p a (b g t w) -> p (a b) t g w", b=2, t=4, w=4),
                     )
                     nc.vector.tensor_copy(
-                        out=w2_planes[:].rearrange("p a (b t q) -> p (a b) t q", b=2, t=4),
-                        in_=w2_raw_planes[:].rearrange("p a (b q t) -> p (a b) t q", b=2, t=4),
+                        out=w2_planes[:].bitcast(I32).rearrange("p a (b t g w) -> p (a b) t g w", b=2, t=4, w=2),
+                        in_=w2_raw_planes[:].bitcast(I32).rearrange("p a (b g t w) -> p (a b) t g w", b=2, t=4, w=2),
                     )
-                if s in (5, 6):
-                    quantize_w3(s - 5, load_w3(s - 5))
+                if s == 7:
+                    for b in range(2):
+                        quantize_w3(b, w3_raws[b])
                 rewrite_page(s, make_h(s))
 
         tail = ctx.enter_context(tc.tile_pool(name="tail", bufs=1))
         out_rows = out.rearrange("(u p) j -> p u j", p=P)
 
-        def make_x(j0, n):
+        def pick(picked, windows, offsets, a, j0):
+            for t in range(4):
+                nc.vector.tensor_tensor(
+                    picked[:, t, :],
+                    windows[t][:].indirect(offsets[:, j0 // 16 : (j0 + GROUP) // 16]),
+                    levels[4 * a + t][:, j0 : j0 + GROUP],
+                    ALU.subtract,
+                )
+
+        def pick_group(g):
+            j0 = GROUP * g
+            old_lower = tail.tile([P, 4, GROUP], F32, name="old_lower")
+            picked = tail.tile([P, 2, 4, GROUP], F32, name="picked", tag=f"ring{g % 2}", align_bytes=64)
+            pick(old_lower, untouched, list4, 0, j0)
+            for a in range(2):
+                pick(picked[:, a], pages[4 * a : 4 * a + 4], list3, a, j0)
+            return [old_lower[:], old_upper[:, :, j0 : j0 + GROUP]], [picked[:, 0], picked[:, 1]]
+
+        def make_x(olds, news, cols):
+            n = cols.stop - cols.start
             codes = tail.tile([P, 2, n], U32, name="x_codes", bufs=2, align_bytes=64)
             plane = tail.tile([P, 2, n], U8, name="x_plane", bufs=2, align_bytes=64)
             grouped = tail.tile([P, 2, 4 * n], BF16, name="x_grouped", bufs=2, align_bytes=64)
-            news = []
-            for a in range(2):
-                new = tail.tile([P, 4, n], F32, name="new", bufs=3)
-                for t in range(4):
-                    s = 4 * a + t
-                    nc.vector.tensor_tensor(
-                        new[:, t, :],
-                        pages[s][:].indirect(list3[:, j0 // 16 : (j0 + n) // 16]),
-                        levels[s][:, j0 : j0 + n],
-                        ALU.subtract,
-                    )
-                news.append(new)
             for a in range(2):
                 nc.vector.tensor_tensor(
-                    grouped[:, a, :].rearrange("p (c i t) -> p c t i", t=4, i=4),
-                    news[a][:].rearrange("p t (c i) -> p c t i", i=4),
-                    olds[a][:, :, j0 : j0 + n].rearrange("p t (c i) -> p c t i", i=4),
+                    grouped[:, a, :].rearrange("p (c i t) -> p c t i", t=4, i=2),
+                    news[a][:, :, cols].rearrange("p t (c i) -> p c t i", i=2),
+                    olds[a][:, :, cols].rearrange("p t (c i) -> p c t i", i=2),
                     ALU.max,
                 )
             for a in range(2):
                 nc.vector.quantize_mx(out=codes[:, a, :].bitcast(FP8X4), scales=plane[:, a, :], in_=grouped[:, a, :])
             return codes, plane
 
-        def make_d(n, codes, plane, on_vector):
+        def gelu_half(b, act, x_codes, x_plane):
+            n = act.shape[2]
             per_bank = BANK // n
-            groups = []
-            for b in range(2):
-                act = tail.tile([P, 4, n], F32, name="act", bufs=2)
-                for t0 in range(0, 4, per_bank):
-                    acc = psum.tile([P, per_bank, n], F32, name="acc2", tag="wide", bufs=5)
-                    for u in range(per_bank):
-                        c0 = 512 * b + P * (t0 + u)
-                        for a in range(2):
-                            nc.tensor.matmul_mx(
-                                out=acc[:, u, :],
-                                lhsT=w2_codes[:, a, 2 * c0 : 2 * (c0 + P)].bitcast(FP4X4),
-                                lhsT_scale=w2_planes[:, a, c0 : c0 + P],
-                                rhs=codes[:, a, :].bitcast(FP8X4),
-                                rhs_scale=plane[:, a, :],
-                                start=(a == 0),
-                                stop=(a == 1),
-                            )
-                    nc.scalar.activation(out=act[:, t0 : t0 + per_bank, :], in_=acc[:], func=ACT.Gelu_apprx_tanh)
-                grouped = tail.tile([P, 4 * n], BF16, name="d_grouped", bufs=3, align_bytes=64)
-                if on_vector:
-                    nc.vector.tensor_tensor(
-                        grouped[:].rearrange("p (c i t) -> p c t i", t=4, i=4),
-                        act[:].rearrange("p t (c i) -> p c t i", i=4),
-                        mgain_sb[:, b, :].unsqueeze(1).unsqueeze(3).to_broadcast([P, n // 4, 4, 4]),
-                        ALU.mult,
-                    )
-                else:
-                    scaled = tail.tile([P, 4, n], BF16, name="scaled", bufs=2)
-                    for t in range(4):
-                        nc.scalar.activation(
-                            out=scaled[:, t, :], in_=act[:, t, :], func=ACT.Copy, scale=mgain_sb[:, b, t : t + 1]
+            for t0 in range(0, 4, per_bank):
+                acc = psum.tile([P, per_bank, n], F32, name="acc2", tag="wide", bufs=4)
+                for u in range(per_bank):
+                    c0 = 512 * b + P * (t0 + u)
+                    for a in range(2):
+                        nc.tensor.matmul_mx(
+                            out=acc[:, u, :],
+                            lhsT=w2_codes[:, a, 2 * c0 : 2 * (c0 + P)].bitcast(FP4X4),
+                            lhsT_scale=w2_planes[:, a, c0 : c0 + P],
+                            rhs=x_codes[:, a, :].bitcast(FP8X4),
+                            rhs_scale=x_plane[:, a, :],
+                            start=(a == 0),
+                            stop=(a == 1),
                         )
-                    nc.scalar.copy(
-                        out=grouped[:].rearrange("p (c i t) -> p c t i", t=4, i=8),
-                        in_=scaled[:].rearrange("p t (c i) -> p c t i", i=8),
-                    )
-                groups.append(grouped)
-            return groups
+                nc.scalar.activation(out=act[:, t0 : t0 + per_bank, :], in_=acc[:], func=ACT.Gelu_apprx_tanh)
 
-        def finish(j0, n, groups):
-            codes = tail.tile([P, 2, n], U32, name="d_codes", bufs=2, align_bytes=64)
-            plane = tail.tile([P, 2, n], U8, name="d_plane", bufs=2, align_bytes=64)
+        def weave_on_scalar(b, act, grouped):
+            for t in range(4):
+                nc.scalar.activation(out=act[:, t, :], in_=act[:, t, :], func=ACT.Copy, scale=mgain_sb[b][:, t : t + 1])
+            nc.scalar.copy(
+                out=grouped[:, b, :].rearrange("p (c i t) -> p c t i", t=4, i=2),
+                in_=act.rearrange("p t (c i) -> p c t i", i=2),
+            )
+
+        def weave_on_vector(b, act, grouped):
+            n = act.shape[2]
+            nc.vector.tensor_tensor(
+                grouped[:, b, :].rearrange("p (c i t) -> p c t i", t=4, i=2),
+                act.rearrange("p t (c i) -> p c t i", i=2),
+                mgain_sb[b][:].unsqueeze(1).unsqueeze(3).to_broadcast([P, n // 2, 4, 2]),
+                ALU.mult,
+            )
+
+        def quantize_d(grouped):
+            n = grouped.shape[2] // 4
+            codes = tail.tile([P, 2, n], U32, name="d_codes", bufs=3, align_bytes=64)
+            plane = tail.tile([P, 2, n], U8, name="d_plane", bufs=3, align_bytes=64)
             for b in range(2):
-                nc.vector.quantize_mx(out=codes[:, b, :].bitcast(FP8X4), scales=plane[:, b, :], in_=groups[b][:])
-            result = tail.tile([P, 3, n], F32, name="result", bufs=2)
+                nc.vector.quantize_mx(out=codes[:, b, :].bitcast(FP8X4), scales=plane[:, b, :], in_=grouped[:, b, :])
+            return codes, plane
+
+        def finish(j0, result, codes, plane, copy):
+            n = result.shape[2]
             per_bank = BANK // n
             for u0 in range(0, 3, per_bank):
                 count = min(per_bank, 3 - u0)
                 acc = psum.tile([P, count, n], F32, name="acc3", tag="scores", bufs=3)
-                for u in range(count):
-                    c0 = P * (u0 + u)
-                    for b in range(2):
+                for b in range(2):
+                    for u in range(count):
+                        c0 = P * (u0 + u)
                         nc.tensor.matmul_mx(
                             out=acc[:, u, :],
                             lhsT=w3_codes[b][:, c0 : c0 + P].bitcast(FP8X4),
                             lhsT_scale=w3_planes[b][:, c0 : c0 + P],
                             rhs=codes[:, b, :].bitcast(FP8X4),
                             rhs_scale=plane[:, b, :],
-                            start=(b == 0),
-                            stop=(b == 1),
+                            start=(b == 0 and u == 0),
+                            stop=(b == 1 and u == count - 1),
                         )
-                nc.scalar.copy(out=result[:, u0 : u0 + count, :], in_=acc[:])
-            nc.sync.dma_start(out=out_rows[:, :, j0 : j0 + n], in_=result[:])
+                copy(out=result[:, u0 : u0 + count, :], in_=acc[:])
+            nc.sync.dma_start(out=out_rows[:, :, j0 : j0 + n], in_=result)
 
-        starts = [sum(CHUNKS[:c]) for c in range(len(CHUNKS))]
-        pending = None
-        for c, n in enumerate(CHUNKS):
-            codes, plane = make_x(starts[c], n)
-            if pending is not None:
-                finish(*pending)
-            groups = make_d(n, codes, plane, c == len(CHUNKS) - 1)
-            pending = (starts[c], n, groups)
-        finish(*pending)
+        groups = PJ // GROUP
+        previous = None
+        for g in range(groups - 1):
+            olds, news = pick_group(g)
+            x_codes, x_plane = make_x(olds, news, slice(0, GROUP))
+            if g > 0:
+                d_codes, d_plane = quantize_d(previous)
+            grouped = tail.tile([P, 2, 4 * GROUP], BF16, name="d_grouped", tag=f"ring{g % 2}", align_bytes=64)
+            for b in range(2):
+                act = tail.tile([P, 4, GROUP], F32, name="act", tag=f"act{b}")
+                gelu_half(b, act[:], x_codes, x_plane)
+                weave_on_scalar(b, act[:], grouped)
+                if g > 0 and b == 0:
+                    result = tail.tile([P, 3, GROUP], F32, name="result", tag="act0")
+                    finish(GROUP * (g - 1), result[:], d_codes, d_plane, nc.scalar.copy)
+            previous = grouped
+
+        j0 = PJ - GROUP
+        piece = GROUP // 2
+        olds, news = pick_group(groups - 1)
+        halves = [make_x(olds, news, slice(piece * k, piece * (k + 1))) for k in range(2)]
+        d_codes, d_plane = quantize_d(previous)
+        acts = [tail.tile([P, 2, 4, piece], F32, name="act", tag=f"act{b}") for b in range(2)]
+        results = tail.tile([P, 3, 2 * GROUP], F32, name="results")
+        woven = tail.tile([P, 2, 2, 4 * piece], BF16, name="woven", align_bytes=64)
+        last = []
+        for k in range(2):
+            for b in range(2):
+                gelu_half(b, acts[b][:, k], *halves[k])
+                weave_on_vector(b, acts[b][:, k], woven[:, k])
+            last.append(quantize_d(woven[:, k]))
+        finish(j0 - GROUP, results[:, :, 0:GROUP], d_codes, d_plane, nc.scalar.copy)
+        for k in range(2):
+            c0 = GROUP + piece * k
+            finish(j0 + piece * k, results[:, :, c0 : c0 + piece], *last[k], [nc.scalar.copy, nc.vector.tensor_copy][k])

@@ -18,8 +18,11 @@ ACT = mybir.ActivationFunctionType
 
 P = 128
 BANK = 512
+PASS = 512
 GROUP = 256
+EARLY = PJ - GROUP
 FIRST_PIECES = [(0, 256), (256, 512), (512, 1024)]
+QUADRANTS = (0, 2, 1, 3)
 
 
 def tile_list_pool_breeding_scores_kernel(
@@ -37,7 +40,7 @@ def tile_list_pool_breeding_scores_kernel(
         pages = [keep.tile([P, T2], F32, name=f"page{s}") for s in range(8)]
         untouched = [keep.tile([P, T2], F32, name=f"untouched{t}") for t in range(4)]
         levels = [keep.tile([P, PJ], F32, name=f"level{s}") for s in range(8)]
-        old_upper = keep.tile([P, 4, PJ], F32, name="old_upper")
+        old_upper = keep.tile([P, 4, EARLY], F32, name="old_upper")
         gain_sb = keep.tile([P, 2, 4], F32, name="gain_sb")
         mgain_sb = [keep.tile([P, 4], F32, name=f"mgain_sb{b}") for b in range(2)]
         w2_codes = keep.tile([P, 2, 2 * M], U8, name="w2_codes", align_bytes=64)
@@ -61,19 +64,19 @@ def tile_list_pool_breeding_scores_kernel(
             wgs_rest = head.tile([P, 2, S], F32, name="wgs_rest")
             w2_raw = head.tile([P, 2, 2 * M], U8, name="w2_raw")
             w2_raw_planes = head.tile([P, 2, M], U8, name="w2_raw_planes")
-            w1_codes = [head.tile([P, 512], U32, name=f"w1_codes{a}", align_bytes=64) for a in range(2)]
-            w1_planes = [head.tile([P, 512], U8, name=f"w1_planes{a}", align_bytes=64) for a in range(2)]
+            w1_codes = [head.tile([P, PASS], U32, name=f"w1_codes{a}", align_bytes=64) for a in range(2)]
+            w1_planes = [head.tile([P, PASS], U8, name=f"w1_planes{a}", align_bytes=64) for a in range(2)]
 
             def load_w1(a):
-                raw = head.tile([P, 4, 512], F32, name="w1_raw", tag="raw", bufs=2)
-                nc.sync.dma_start(out=raw[:], in_=w1[:, 512 * a : 512 * (a + 1)].rearrange("(p j) c -> p j c", j=4))
+                raw = head.tile([P, 4, PASS], F32, name="w1_raw", tag="raw", bufs=2)
+                nc.sync.dma_start(out=raw[:], in_=w1[:, PASS * a : PASS * (a + 1)].rearrange("(p i) c -> p i c", i=4))
                 return raw
 
             def quantize_w1(a, raw, t0, t1):
-                grouped = head.tile([P, (t1 - t0) * 512], BF16, name=f"w1_grouped{t1 - t0}", align_bytes=64)
+                grouped = head.tile([P, (t1 - t0) * 4 * P], BF16, name=f"w1_grouped{t1 - t0}", align_bytes=64)
                 nc.scalar.copy(
-                    out=grouped[:].rearrange("p (t m j) -> p m t j", m=P, j=4),
-                    in_=raw[:].rearrange("p j (m t) -> p m t j", t=4)[:, :, t0:t1, :],
+                    out=grouped[:].rearrange("p (t q i) -> p q t i", q=P, i=4),
+                    in_=raw[:].rearrange("p i (q t) -> p q t i", t=4)[:, :, t0:t1, :],
                 )
                 cols = slice(P * t0, P * t1)
                 nc.vector.quantize_mx(out=w1_codes[a][:, cols].bitcast(FP8X4), scales=w1_planes[a][:, cols], in_=grouped[:])
@@ -89,15 +92,22 @@ def tile_list_pool_breeding_scores_kernel(
             def quantize_w3(b, raw):
                 grouped = head.tile([P, 4 * N], BF16, name="w3_grouped", bufs=2, align_bytes=64)
                 nc.scalar.copy(
-                    out=grouped[:].rearrange("p (c i t) -> p c t i", t=4, i=4),
-                    in_=raw[:].rearrange("p t (c i) -> p c t i", i=4),
+                    out=grouped[:].rearrange("p (c e t) -> p c t e", t=4, e=4),
+                    in_=raw[:].rearrange("p t (c e) -> p c t e", e=4),
                 )
                 nc.vector.quantize_mx(out=w3_codes[b][:].bitcast(FP8X4), scales=w3_planes[b][:], in_=grouped[:])
+
+            def deal_w2():
+                for dealt, raw, words in ((w2_codes, w2_raw, 4), (w2_planes, w2_raw_planes, 2)):
+                    nc.vector.tensor_copy(
+                        out=dealt[:].bitcast(I32).rearrange("p a (b t g w) -> p (a b) t g w", b=2, t=4, w=words),
+                        in_=raw[:].bitcast(I32).rearrange("p a (b g t w) -> p (a b) t g w", b=2, t=4, w=words),
+                    )
 
             def make_h(s):
                 a, t = divmod(s, 4)
                 h = head.tile([P, S], F32, name="h", tag="h", bufs=3)
-                for j0, j1 in (FIRST_PIECES if s == 0 else [(0, BANK), (BANK, S)]):
+                for j0, j1 in FIRST_PIECES if s == 0 else [(0, BANK), (BANK, S)]:
                     cols = slice(j0, j1)
                     acc = psum.tile([P, j1 - j0], F32, name="acc1")
                     nc.tensor.matmul_mx(
@@ -116,9 +126,11 @@ def tile_list_pool_breeding_scores_kernel(
             def rewrite_page(s, h):
                 a, t = divmod(s, 4)
                 if a == 1:
-                    nc.vector.tensor_tensor(old_upper[:, t, :], pages[s][:].indirect(list4[:]), levels[s][:], ALU.subtract)
+                    nc.vector.tensor_tensor(
+                        old_upper[:, t, :], pages[s][:].indirect(list4[:, 0 : EARLY // 16]), levels[s][:, 0:EARLY], ALU.subtract
+                    )
                 weights = [wgs_first[:], wgs_second[:], wgs_rest[:, 0, :], wgs_rest[:, 1, :]][t]
-                for j0, j1 in (FIRST_PIECES if s == 0 else [(0, S)]):
+                for j0, j1 in FIRST_PIECES if s == 0 else [(0, S)]:
                     nc.vector.tensor_tensor(
                         pages[s][:].indirect(list2[:, j0 // 16 : j1 // 16]), h[:, j0:j1], weights[:, j0:j1], ALU.mult
                     )
@@ -139,20 +151,20 @@ def tile_list_pool_breeding_scores_kernel(
             w1_raw0 = load_w1(0)
             nc.sync.dma_start(out=pages[0][:], in_=page_rows[0, 0])
             nc.sync.dma_start(list2[:], offs2)
-            for q in (0, 2, 1, 3):
+            for q in QUADRANTS:
                 nc.sync.dma_start(out=wgs_first[32 * q : 32 * (q + 1), :], in_=wgs_rows[:, 0, :])
             nc.sync.dma_start(out=pages[1][:], in_=page_rows[0, 1])
-            for q in (0, 2, 1, 3):
+            for q in QUADRANTS:
                 nc.sync.dma_start(out=wgs_second[32 * q : 32 * (q + 1), :], in_=wgs_rows[:, 1, :])
             nc.sync.dma_start(out=pages[2][:], in_=page_rows[0, 2])
-            for q in (0, 2, 1, 3):
+            for q in QUADRANTS:
                 nc.sync.dma_start(out=wgs_rest[32 * q : 32 * (q + 1), :, :], in_=wgs_rows[:, 2:4, :])
             w1_raw1 = load_w1(1)
             nc.sync.dma_start(out=pages[3][:], in_=page_rows[0, 3])
             nc.sync.dma_start(list4[:], offs4)
-            for s in range(4, 8):
-                nc.sync.dma_start(out=pages[s][:], in_=page_rows[1, s - 4])
-                nc.sync.dma_start(out=levels[s][:], in_=level_rows[1, s - 4])
+            for t in range(4):
+                nc.sync.dma_start(out=pages[4 + t][:], in_=page_rows[1, t])
+                nc.sync.dma_start(out=levels[4 + t][:], in_=level_rows[1, t])
             for a in range(2):
                 nc.sync.dma_start(out=w2_raw[:, a, :].bitcast(I32), in_=w2_words[a].bitcast(I32))
             for q in range(4):
@@ -170,25 +182,23 @@ def tile_list_pool_breeding_scores_kernel(
             nc.vector.tensor_copy(v_plane[:], tab_plane[:].indirect(list1[:]))
             quantize_w1(0, w1_raw0, 0, 1)
             quantize_w1(0, w1_raw0, 1, 4)
-            for s in range(8):
-                if s == 2:
-                    quantize_w1(1, w1_raw1, 0, 4)
-                if s == 6:
-                    nc.vector.tensor_copy(
-                        out=w2_codes[:].bitcast(I32).rearrange("p a (b t g w) -> p (a b) t g w", b=2, t=4, w=4),
-                        in_=w2_raw[:].bitcast(I32).rearrange("p a (b g t w) -> p (a b) t g w", b=2, t=4, w=4),
-                    )
-                    nc.vector.tensor_copy(
-                        out=w2_planes[:].bitcast(I32).rearrange("p a (b t g w) -> p (a b) t g w", b=2, t=4, w=2),
-                        in_=w2_raw_planes[:].bitcast(I32).rearrange("p a (b g t w) -> p (a b) t g w", b=2, t=4, w=2),
-                    )
-                if s == 7:
-                    for b in range(2):
-                        quantize_w3(b, w3_raws[b])
+            for s in range(2):
                 rewrite_page(s, make_h(s))
+            quantize_w1(1, w1_raw1, 0, 4)
+            for s in range(2, 6):
+                rewrite_page(s, make_h(s))
+            deal_w2()
+            rewrite_page(6, make_h(6))
+            for b in range(2):
+                quantize_w3(b, w3_raws[b])
+            rewrite_page(7, make_h(7))
 
         tail = ctx.enter_context(tc.tile_pool(name="tail", bufs=1))
         out_rows = out.rearrange("(u p) j -> p u j", p=P)
+
+        reloaded = [tail.tile([P, T2], F32, name=f"reloaded{t}") for t in range(4)]
+        for t in range(4):
+            nc.sync.dma_start(out=reloaded[t][:], in_=page_rows[1, t])
 
         def pick(picked, windows, offsets, a, j0):
             for t in range(4):
@@ -201,27 +211,32 @@ def tile_list_pool_breeding_scores_kernel(
 
         def pick_group(g):
             j0 = GROUP * g
-            old_lower = tail.tile([P, 4, GROUP], F32, name="old_lower")
-            picked = tail.tile([P, 2, 4, GROUP], F32, name="picked", tag=f"ring{g % 2}", align_bytes=64)
+            late = j0 >= EARLY
+            old_lower = tail.tile([P, 4, GROUP], F32, name="old_lower", align_bytes=64)
+            picked = tail.tile([P, 3 if late else 2, 4, GROUP], F32, name="picked", tag=f"ring{g % 2}", align_bytes=64)
             pick(old_lower, untouched, list4, 0, j0)
             for a in range(2):
                 pick(picked[:, a], pages[4 * a : 4 * a + 4], list3, a, j0)
-            return [old_lower[:], old_upper[:, :, j0 : j0 + GROUP]], [picked[:, 0], picked[:, 1]]
+            if late:
+                pick(picked[:, 2], reloaded, list4, 1, j0)
+            return [old_lower[:], picked[:, 2] if late else old_upper[:, :, j0 : j0 + GROUP]], [picked[:, 0], picked[:, 1]]
 
-        def make_x(olds, news, cols):
+        def by_slots(planar):
+            return planar.rearrange("p t (c e) -> p c t e", e=2)
+
+        def by_words(woven):
+            return woven.rearrange("p (c e t) -> p c t e", t=4, e=2)
+
+        def make_x(olds, news, cols, x_woven):
             n = cols.stop - cols.start
             codes = tail.tile([P, 2, n], U32, name="x_codes", bufs=2, align_bytes=64)
             plane = tail.tile([P, 2, n], U8, name="x_plane", bufs=2, align_bytes=64)
-            grouped = tail.tile([P, 2, 4 * n], BF16, name="x_grouped", bufs=2, align_bytes=64)
             for a in range(2):
                 nc.vector.tensor_tensor(
-                    grouped[:, a, :].rearrange("p (c i t) -> p c t i", t=4, i=2),
-                    news[a][:, :, cols].rearrange("p t (c i) -> p c t i", i=2),
-                    olds[a][:, :, cols].rearrange("p t (c i) -> p c t i", i=2),
-                    ALU.max,
+                    by_words(x_woven[:, a, :]), by_slots(news[a][:, :, cols]), by_slots(olds[a][:, :, cols]), ALU.max
                 )
             for a in range(2):
-                nc.vector.quantize_mx(out=codes[:, a, :].bitcast(FP8X4), scales=plane[:, a, :], in_=grouped[:, a, :])
+                nc.vector.quantize_mx(out=codes[:, a, :].bitcast(FP8X4), scales=plane[:, a, :], in_=x_woven[:, a, :])
             return codes, plane
 
         def gelu_half(b, act, x_codes, x_plane):
@@ -230,7 +245,7 @@ def tile_list_pool_breeding_scores_kernel(
             for t0 in range(0, 4, per_bank):
                 acc = psum.tile([P, per_bank, n], F32, name="acc2", tag="wide", bufs=4)
                 for u in range(per_bank):
-                    c0 = 512 * b + P * (t0 + u)
+                    c0 = PASS * b + P * (t0 + u)
                     for a in range(2):
                         nc.tensor.matmul_mx(
                             out=acc[:, u, :],
@@ -243,36 +258,28 @@ def tile_list_pool_breeding_scores_kernel(
                         )
                 nc.scalar.activation(out=act[:, t0 : t0 + per_bank, :], in_=acc[:], func=ACT.Gelu_apprx_tanh)
 
-        def weave_on_scalar(b, act, grouped):
+        def weave_on_scalar(b, act, d_woven):
             for t in range(4):
                 nc.scalar.activation(out=act[:, t, :], in_=act[:, t, :], func=ACT.Copy, scale=mgain_sb[b][:, t : t + 1])
-            nc.scalar.copy(
-                out=grouped[:, b, :].rearrange("p (c i t) -> p c t i", t=4, i=2),
-                in_=act.rearrange("p t (c i) -> p c t i", i=2),
-            )
+            nc.scalar.copy(out=by_words(d_woven[:, b, :]), in_=by_slots(act))
 
-        def weave_on_vector(b, act, grouped):
-            n = act.shape[2]
-            nc.vector.tensor_tensor(
-                grouped[:, b, :].rearrange("p (c i t) -> p c t i", t=4, i=2),
-                act.rearrange("p t (c i) -> p c t i", i=2),
-                mgain_sb[b][:].unsqueeze(1).unsqueeze(3).to_broadcast([P, n // 2, 4, 2]),
-                ALU.mult,
-            )
+        def weave_on_vector(b, act, d_woven):
+            gains = mgain_sb[b][:].unsqueeze(1).unsqueeze(3).to_broadcast([P, act.shape[2] // 2, 4, 2])
+            nc.vector.tensor_tensor(by_words(d_woven[:, b, :]), by_slots(act), gains, ALU.mult)
 
-        def quantize_d(grouped):
-            n = grouped.shape[2] // 4
+        def quantize_d(d_woven):
+            n = d_woven.shape[2] // 4
             codes = tail.tile([P, 2, n], U32, name="d_codes", bufs=3, align_bytes=64)
             plane = tail.tile([P, 2, n], U8, name="d_plane", bufs=3, align_bytes=64)
             for b in range(2):
-                nc.vector.quantize_mx(out=codes[:, b, :].bitcast(FP8X4), scales=plane[:, b, :], in_=grouped[:, b, :])
+                nc.vector.quantize_mx(out=codes[:, b, :].bitcast(FP8X4), scales=plane[:, b, :], in_=d_woven[:, b, :])
             return codes, plane
 
-        def finish(j0, result, codes, plane, copy):
+        def finish(j0, result, d_codes, d_plane, copy):
             n = result.shape[2]
             per_bank = BANK // n
-            for u0 in range(0, 3, per_bank):
-                count = min(per_bank, 3 - u0)
+            for u0 in range(0, N // P, per_bank):
+                count = min(per_bank, N // P - u0)
                 acc = psum.tile([P, count, n], F32, name="acc3", tag="scores", bufs=3)
                 for b in range(2):
                     for u in range(count):
@@ -281,8 +288,8 @@ def tile_list_pool_breeding_scores_kernel(
                             out=acc[:, u, :],
                             lhsT=w3_codes[b][:, c0 : c0 + P].bitcast(FP8X4),
                             lhsT_scale=w3_planes[b][:, c0 : c0 + P],
-                            rhs=codes[:, b, :].bitcast(FP8X4),
-                            rhs_scale=plane[:, b, :],
+                            rhs=d_codes[:, b, :].bitcast(FP8X4),
+                            rhs_scale=d_plane[:, b, :],
                             start=(b == 0 and u == 0),
                             stop=(b == 1 and u == count - 1),
                         )
@@ -293,34 +300,36 @@ def tile_list_pool_breeding_scores_kernel(
         previous = None
         for g in range(groups - 1):
             olds, news = pick_group(g)
-            x_codes, x_plane = make_x(olds, news, slice(0, GROUP))
+            x_woven = tail.tile([P, 2, 4 * GROUP], BF16, name="x_woven", align_bytes=64)
+            x_codes, x_plane = make_x(olds, news, slice(0, GROUP), x_woven)
             if g > 0:
                 d_codes, d_plane = quantize_d(previous)
-            grouped = tail.tile([P, 2, 4 * GROUP], BF16, name="d_grouped", tag=f"ring{g % 2}", align_bytes=64)
+            d_woven = tail.tile([P, 2, 4 * GROUP], BF16, name="d_woven", tag=f"ring{g % 2}", align_bytes=64)
             for b in range(2):
                 act = tail.tile([P, 4, GROUP], F32, name="act", tag=f"act{b}")
                 gelu_half(b, act[:], x_codes, x_plane)
-                weave_on_scalar(b, act[:], grouped)
+                weave_on_scalar(b, act[:], d_woven)
                 if g > 0 and b == 0:
-                    result = tail.tile([P, 3, GROUP], F32, name="result", tag="act0")
+                    result = tail.tile([P, N // P, GROUP], F32, name="result", tag="act0")
                     finish(GROUP * (g - 1), result[:], d_codes, d_plane, nc.scalar.copy)
-            previous = grouped
+            previous = d_woven
 
         j0 = PJ - GROUP
         piece = GROUP // 2
         olds, news = pick_group(groups - 1)
-        halves = [make_x(olds, news, slice(piece * k, piece * (k + 1))) for k in range(2)]
         d_codes, d_plane = quantize_d(previous)
+        results = tail.tile([P, N // P, 2 * GROUP], F32, name="results")
+        finish(j0 - GROUP, results[:, :, 0:GROUP], d_codes, d_plane, nc.scalar.copy)
+        x_last = tail.tile([P, 2, 2, 4 * piece], BF16, name="x_last", tag=f"ring{groups % 2}", align_bytes=64)
+        x_pieces = [make_x(olds, news, slice(piece * k, piece * (k + 1)), x_last[:, k]) for k in range(2)]
         acts = [tail.tile([P, 2, 4, piece], F32, name="act", tag=f"act{b}") for b in range(2)]
-        results = tail.tile([P, 3, 2 * GROUP], F32, name="results")
-        woven = tail.tile([P, 2, 2, 4 * piece], BF16, name="woven", align_bytes=64)
-        last = []
+        d_last = tail.tile([P, 2, 2, 4 * piece], BF16, name="d_last", tag="old_lower", align_bytes=64)
+        d_pieces = []
         for k in range(2):
             for b in range(2):
-                gelu_half(b, acts[b][:, k], *halves[k])
-                weave_on_vector(b, acts[b][:, k], woven[:, k])
-            last.append(quantize_d(woven[:, k]))
-        finish(j0 - GROUP, results[:, :, 0:GROUP], d_codes, d_plane, nc.scalar.copy)
-        for k in range(2):
+                gelu_half(b, acts[b][:, k], *x_pieces[k])
+                weave_on_vector(b, acts[b][:, k], d_last[:, k])
+            d_pieces.append(quantize_d(d_last[:, k]))
+        for k, copy in enumerate((nc.scalar.copy, nc.vector.tensor_copy)):
             c0 = GROUP + piece * k
-            finish(j0 + piece * k, results[:, :, c0 : c0 + piece], *last[k], [nc.scalar.copy, nc.vector.tensor_copy][k])
+            finish(j0 + piece * k, results[:, :, c0 : c0 + piece], *d_pieces[k], copy)

from contextlib import ExitStack

import concourse.mybir as mybir

K, H, M, N, T, S, T2, PJ = 512, 1024, 1024, 384, 2048, 1024, 2048, 1024
FLOPS = 2 * (K * H * S + H * M * PJ + M * N * PJ)

F32 = mybir.dt.float32
BF16 = mybir.dt.bfloat16
I32 = mybir.dt.int32
U32 = mybir.dt.uint32
U16 = mybir.dt.uint16
U8 = mybir.dt.uint8
FP8X4 = mybir.dt.float8_e4m3fn_x4
FP4X4 = mybir.dt.float4_e2m1fn_x4
ALU = mybir.AluOpType
ACT = mybir.ActivationFunctionType

P = 128
BANK = 512
PASS = 512
GROUP = 256
EARLY = PJ - GROUP
FIRST_PIECES = [(0, 256), (256, 512), (512, 1024)]
QUADRANTS = (0, 2, 1, 3)


def tile_list_pool_breeding_scores_kernel(
    tc, tab_words, tab_scales, offs, offs2, offs3, offs4, w1, gain, wgs, page0, level, w2_words, w2_scales, mgain, w3, out
):
    nc = tc.nc
    with ExitStack() as ctx:
        keep = ctx.enter_context(tc.tile_pool(name="keep", bufs=1))
        psum = ctx.enter_context(tc.psum_pool(name="psum", bufs=1))

        list1 = keep.tile([P, S // 16], U16, name="list1")
        list2 = keep.tile([P, S // 16], U16, name="list2")
        list3 = keep.tile([P, PJ // 16], U16, name="list3")
        list4 = keep.tile([P, PJ // 16], U16, name="list4")
        pages = [keep.tile([P, T2], F32, name=f"page{s}") for s in range(8)]
        untouched = [keep.tile([P, T2], F32, name=f"untouched{t}") for t in range(4)]
        levels = [keep.tile([P, PJ], F32, name=f"level{s}") for s in range(8)]
        old_upper = keep.tile([P, 4, EARLY], F32, name="old_upper")
        gain_sb = keep.tile([P, 2, 4], F32, name="gain_sb")
        mgain_sb = [keep.tile([P, 4], F32, name=f"mgain_sb{b}") for b in range(2)]
        w2_codes = keep.tile([P, 2, 2 * M], U8, name="w2_codes", align_bytes=64)
        w2_planes = keep.tile([P, 2, M], U8, name="w2_planes", align_bytes=64)
        w3_codes = [keep.tile([P, N], U32, name=f"w3_codes{b}", align_bytes=64) for b in range(2)]
        w3_planes = [keep.tile([P, N], U8, name=f"w3_planes{b}", align_bytes=64) for b in range(2)]

        page_rows = page0.rearrange("(a p t) c -> a t p c", a=2, t=4)
        level_rows = level.rearrange("(a p t) c -> a t p c", a=2, t=4)
        wgs_rows = wgs.rearrange("(p t) j -> p t j", t=4)
        w3_rows = w3.rearrange("(b g t i) n -> b i g t n", b=2, t=4, i=8)
        mgain_rows = mgain.rearrange("(b g t i) -> b i g t", b=2, t=4, i=8)

        with tc.tile_pool(name="head", bufs=1) as head:
            tab_sb = head.tile([P, T], I32, name="tab_sb")
            tab_plane = head.tile([P, T], U8, name="tab_plane")
            v_codes = head.tile([P, S], U32, name="v_codes", align_bytes=64)
            v_plane = head.tile([P, S], U8, name="v_plane", align_bytes=64)
            wgs_first = head.tile([P, S], F32, name="wgs_first")
            wgs_second = head.tile([P, S], F32, name="wgs_second")
            wgs_rest = head.tile([P, 2, S], F32, name="wgs_rest")
            w2_raw = head.tile([P, 2, 2 * M], U8, name="w2_raw")
            w2_raw_planes = head.tile([P, 2, M], U8, name="w2_raw_planes")
            w1_codes = [head.tile([P, PASS], U32, name=f"w1_codes{a}", align_bytes=64) for a in range(2)]
            w1_planes = [head.tile([P, PASS], U8, name=f"w1_planes{a}", align_bytes=64) for a in range(2)]

            def load_w1(a):
                raw = head.tile([P, 4, PASS], F32, name="w1_raw", tag="raw", bufs=2)
                nc.sync.dma_start(out=raw[:], in_=w1[:, PASS * a : PASS * (a + 1)].rearrange("(p i) c -> p i c", i=4))
                return raw

            def quantize_w1(a, raw, t0, t1):
                grouped = head.tile([P, (t1 - t0) * 4 * P], BF16, name=f"w1_grouped{t1 - t0}", align_bytes=64)
                nc.scalar.copy(
                    out=grouped[:].rearrange("p (t q i) -> p q t i", q=P, i=4),
                    in_=raw[:].rearrange("p i (q t) -> p q t i", t=4)[:, :, t0:t1, :],
                )
                cols = slice(P * t0, P * t1)
                nc.vector.quantize_mx(out=w1_codes[a][:, cols].bitcast(FP8X4), scales=w1_planes[a][:, cols], in_=grouped[:])

            def load_w3(b):
                raw = head.tile([P, 4, N], F32, name="w3_raw", tag="raw", bufs=2)
                for i in range(8):
                    nc.sync.dma_start(out=raw[i:P:8, :, :], in_=w3_rows[b, i])
                    with nc.allow_non_contiguous_dma(reason="one gain to a partition and slot"):
                        nc.sync.dma_start(out=mgain_sb[b][i:P:8, :], in_=mgain_rows[b, i])
                return raw

            def quantize_w3(b, raw):
                grouped = head.tile([P, 4 * N], BF16, name="w3_grouped", bufs=2, align_bytes=64)
                nc.scalar.copy(
                    out=grouped[:].rearrange("p (c e t) -> p c t e", t=4, e=4),
                    in_=raw[:].rearrange("p t (c e) -> p c t e", e=4),
                )
                nc.vector.quantize_mx(out=w3_codes[b][:].bitcast(FP8X4), scales=w3_planes[b][:], in_=grouped[:])

            def deal_w2():
                for dealt, raw, words in ((w2_codes, w2_raw, 4), (w2_planes, w2_raw_planes, 2)):
                    nc.vector.tensor_copy(
                        out=dealt[:].bitcast(I32).rearrange("p a (b t g w) -> p (a b) t g w", b=2, t=4, w=words),
                        in_=raw[:].bitcast(I32).rearrange("p a (b g t w) -> p (a b) t g w", b=2, t=4, w=words),
                    )

            def make_h(s):
                a, t = divmod(s, 4)
                h = head.tile([P, S], F32, name="h", tag="h", bufs=3)
                for j0, j1 in FIRST_PIECES if s == 0 else [(0, BANK), (BANK, S)]:
                    cols = slice(j0, j1)
                    acc = psum.tile([P, j1 - j0], F32, name="acc1")
                    nc.tensor.matmul_mx(
                        out=acc[:],
                        lhsT=w1_codes[a][:, P * t : P * (t + 1)].bitcast(FP8X4),
                        lhsT_scale=w1_planes[a][:, P * t : P * (t + 1)],
                        rhs=v_codes[:, cols].bitcast(FP8X4),
                        rhs_scale=v_plane[:, cols],
                        start=True,
                        stop=True,
                    )
                    nc.scalar.activation(out=h[:, cols], in_=acc[:], func=ACT.Tanh)
                    nc.scalar.activation(out=h[:, cols], in_=h[:, cols], func=ACT.Copy, scale=gain_sb[:, a, t : t + 1])
                return h

            def rewrite_page(s, h):
                a, t = divmod(s, 4)
                if a == 1:
                    nc.vector.tensor_tensor(
                        old_upper[:, t, :], pages[s][:].indirect(list4[:, 0 : EARLY // 16]), levels[s][:, 0:EARLY], ALU.subtract
                    )
                weights = [wgs_first[:], wgs_second[:], wgs_rest[:, 0, :], wgs_rest[:, 1, :]][t]
                for j0, j1 in FIRST_PIECES if s == 0 else [(0, S)]:
                    nc.vector.tensor_tensor(
                        pages[s][:].indirect(list2[:, j0 // 16 : j1 // 16]), h[:, j0:j1], weights[:, j0:j1], ALU.mult
                    )

            nc.vector.memset(tab_plane[:].bitcast(I32), 0)

            nc.sync.dma_start(list1[:], offs)
            nc.sync.dma_start(out=gain_sb[:], in_=gain.rearrange("(a p t) -> p a t", a=2, t=4))
            warm = head.tile([P, 1], F32, name="warm")
            nc.gpsimd.memset(warm[:], 0.0)
            nc.scalar.activation(out=warm[:], in_=warm[:], func=ACT.Tanh)
            nc.sync.dma_start(out=tab_sb[:], in_=tab_words[0].rearrange("p n i -> p (n i)").bitcast(I32))
            nc.gpsimd.memset(w2_raw_planes[:].rearrange("p a c -> p (a c)").bitcast(I32), 0)
            for q in range(4):
                nc.sync.dma_start(
                    out=tab_plane[32 * q : 32 * q + 4, :].bitcast(I32), in_=tab_scales[0, 4 * q : 4 * q + 4, :].bitcast(I32)
                )
            w1_raw0 = load_w1(0)
            nc.sync.dma_start(out=pages[0][:], in_=page_rows[0, 0])
            nc.sync.dma_start(list2[:], offs2)
            for q in QUADRANTS:
                nc.sync.dma_start(out=wgs_first[32 * q : 32 * (q + 1), :], in_=wgs_rows[:, 0, :])
            nc.sync.dma_start(out=pages[1][:], in_=page_rows[0, 1])
            for q in QUADRANTS:
                nc.sync.dma_start(out=wgs_second[32 * q : 32 * (q + 1), :], in_=wgs_rows[:, 1, :])
            nc.sync.dma_start(out=pages[2][:], in_=page_rows[0, 2])
            for q in QUADRANTS:
                nc.sync.dma_start(out=wgs_rest[32 * q : 32 * (q + 1), :, :], in_=wgs_rows[:, 2:4, :])
            w1_raw1 = load_w1(1)
            nc.sync.dma_start(out=pages[3][:], in_=page_rows[0, 3])
            nc.sync.dma_start(list4[:], offs4)
            for t in range(4):
                nc.sync.dma_start(out=pages[4 + t][:], in_=page_rows[1, t])
                nc.sync.dma_start(out=levels[4 + t][:], in_=level_rows[1, t])
            for a in range(2):
                nc.sync.dma_start(out=w2_raw[:, a, :].bitcast(I32), in_=w2_words[a].bitcast(I32))
            for q in range(4):
                nc.sync.dma_start(
                    out=w2_raw_planes[32 * q : 32 * q + 4, :, :].bitcast(I32),
                    in_=w2_scales[:, 4 * q : 4 * q + 4, :].rearrange("a r c -> r a c").bitcast(I32),
                )
            w3_raws = [load_w3(b) for b in range(2)]
            nc.sync.dma_start(list3[:], offs3)
            for t in range(4):
                nc.sync.dma_start(out=untouched[t][:], in_=page_rows[0, t])
                nc.sync.dma_start(out=levels[t][:], in_=level_rows[0, t])

            nc.vector.tensor_copy(v_codes[:], tab_sb[:].bitcast(U32).indirect(list1[:]))
            nc.vector.tensor_copy(v_plane[:], tab_plane[:].indirect(list1[:]))
            quantize_w1(0, w1_raw0, 0, 1)
            quantize_w1(0, w1_raw0, 1, 4)
            for s in range(2):
                rewrite_page(s, make_h(s))
            quantize_w1(1, w1_raw1, 0, 4)
            for s in range(2, 6):
                rewrite_page(s, make_h(s))
            deal_w2()
            rewrite_page(6, make_h(6))
            for b in range(2):
                quantize_w3(b, w3_raws[b])
            rewrite_page(7, make_h(7))

        tail = ctx.enter_context(tc.tile_pool(name="tail", bufs=1))
        out_rows = out.rearrange("(u p) j -> p u j", p=P)

        reloaded = [tail.tile([P, T2], F32, name=f"reloaded{t}") for t in range(4)]
        for t in range(4):
            nc.sync.dma_start(out=reloaded[t][:], in_=page_rows[1, t])

        def pick(picked, windows, offsets, a, j0):
            for t in range(4):
                nc.vector.tensor_tensor(
                    picked[:, t, :],
                    windows[t][:].indirect(offsets[:, j0 // 16 : (j0 + GROUP) // 16]),
                    levels[4 * a + t][:, j0 : j0 + GROUP],
                    ALU.subtract,
                )

        def pick_group(g):
            j0 = GROUP * g
            late = j0 >= EARLY
            old_lower = tail.tile([P, 4, GROUP], F32, name="old_lower", align_bytes=64)
            picked = tail.tile([P, 3 if late else 2, 4, GROUP], F32, name="picked", tag=f"ring{g % 2}", align_bytes=64)
            pick(old_lower, untouched, list4, 0, j0)
            for a in range(2):
                pick(picked[:, a], pages[4 * a : 4 * a + 4], list3, a, j0)
            if late:
                pick(picked[:, 2], reloaded, list4, 1, j0)
            return [old_lower[:], picked[:, 2] if late else old_upper[:, :, j0 : j0 + GROUP]], [picked[:, 0], picked[:, 1]]

        def by_slots(planar):
            return planar.rearrange("p t (c e) -> p c t e", e=2)

        def by_words(woven):
            return woven.rearrange("p (c e t) -> p c t e", t=4, e=2)

        def make_x(olds, news, cols, x_woven):
            n = cols.stop - cols.start
            codes = tail.tile([P, 2, n], U32, name="x_codes", bufs=2, align_bytes=64)
            plane = tail.tile([P, 2, n], U8, name="x_plane", bufs=2, align_bytes=64)
            for a in range(2):
                nc.vector.tensor_tensor(
                    by_words(x_woven[:, a, :]), by_slots(news[a][:, :, cols]), by_slots(olds[a][:, :, cols]), ALU.max
                )
            for a in range(2):
                nc.vector.quantize_mx(out=codes[:, a, :].bitcast(FP8X4), scales=plane[:, a, :], in_=x_woven[:, a, :])
            return codes, plane

        def gelu_half(b, act, x_codes, x_plane):
            n = act.shape[2]
            per_bank = BANK // n
            for t0 in range(0, 4, per_bank):
                acc = psum.tile([P, per_bank, n], F32, name="acc2", tag="wide", bufs=4)
                for u in range(per_bank):
                    c0 = PASS * b + P * (t0 + u)
                    for a in range(2):
                        nc.tensor.matmul_mx(
                            out=acc[:, u, :],
                            lhsT=w2_codes[:, a, 2 * c0 : 2 * (c0 + P)].bitcast(FP4X4),
                            lhsT_scale=w2_planes[:, a, c0 : c0 + P],
                            rhs=x_codes[:, a, :].bitcast(FP8X4),
                            rhs_scale=x_plane[:, a, :],
                            start=(a == 0),
                            stop=(a == 1),
                        )
                nc.scalar.activation(out=act[:, t0 : t0 + per_bank, :], in_=acc[:], func=ACT.Gelu_apprx_tanh)

        def weave_on_scalar(b, act, d_woven):
            for t in range(4):
                nc.scalar.activation(out=act[:, t, :], in_=act[:, t, :], func=ACT.Copy, scale=mgain_sb[b][:, t : t + 1])
            nc.scalar.copy(out=by_words(d_woven[:, b, :]), in_=by_slots(act))

        def weave_on_vector(b, act, d_woven):
            gains = mgain_sb[b][:].unsqueeze(1).unsqueeze(3).to_broadcast([P, act.shape[2] // 2, 4, 2])
            nc.vector.tensor_tensor(by_words(d_woven[:, b, :]), by_slots(act), gains, ALU.mult)

        def quantize_d(d_woven):
            n = d_woven.shape[2] // 4
            codes = tail.tile([P, 2, n], U32, name="d_codes", bufs=3, align_bytes=64)
            plane = tail.tile([P, 2, n], U8, name="d_plane", bufs=3, align_bytes=64)
            for b in range(2):
                nc.vector.quantize_mx(out=codes[:, b, :].bitcast(FP8X4), scales=plane[:, b, :], in_=d_woven[:, b, :])
            return codes, plane

        def finish(j0, result, d_codes, d_plane, copy):
            n = result.shape[2]
            per_bank = BANK // n
            for u0 in range(0, N // P, per_bank):
                count = min(per_bank, N // P - u0)
                acc = psum.tile([P, count, n], F32, name="acc3", tag="scores", bufs=3)
                for b in range(2):
                    for u in range(count):
                        c0 = P * (u0 + u)
                        nc.tensor.matmul_mx(
                            out=acc[:, u, :],
                            lhsT=w3_codes[b][:, c0 : c0 + P].bitcast(FP8X4),
                            lhsT_scale=w3_planes[b][:, c0 : c0 + P],
                            rhs=d_codes[:, b, :].bitcast(FP8X4),
                            rhs_scale=d_plane[:, b, :],
                            start=(b == 0 and u == 0),
                            stop=(b == 1 and u == count - 1),
                        )
                copy(out=result[:, u0 : u0 + count, :], in_=acc[:])
            nc.sync.dma_start(out=out_rows[:, :, j0 : j0 + n], in_=result)

        groups = PJ // GROUP
        previous = None
        for g in range(groups - 1):
            olds, news = pick_group(g)
            x_woven = tail.tile([P, 2, 4 * GROUP], BF16, name="x_woven", align_bytes=64)
            x_codes, x_plane = make_x(olds, news, slice(0, GROUP), x_woven)
            if g > 0:
                d_codes, d_plane = quantize_d(previous)
            d_woven = tail.tile([P, 2, 4 * GROUP], BF16, name="d_woven", tag=f"ring{g % 2}", align_bytes=64)
            for b in range(2):
                act = tail.tile([P, 4, GROUP], F32, name="act", tag=f"act{b}")
                gelu_half(b, act[:], x_codes, x_plane)
                weave_on_scalar(b, act[:], d_woven)
                if g > 0 and b == 0:
                    result = tail.tile([P, N // P, GROUP], F32, name="result", tag="act0")
                    finish(GROUP * (g - 1), result[:], d_codes, d_plane, nc.scalar.copy)
            previous = d_woven

        j0 = PJ - GROUP
        piece = GROUP // 2
        olds, news = pick_group(groups - 1)
        d_codes, d_plane = quantize_d(previous)
        results = tail.tile([P, N // P, 2 * GROUP], F32, name="results")
        finish(j0 - GROUP, results[:, :, 0:GROUP], d_codes, d_plane, nc.scalar.copy)
        x_last = tail.tile([P, 2, 2, 4 * piece], BF16, name="x_last", tag=f"ring{groups % 2}", align_bytes=64)
        x_pieces = [make_x(olds, news, slice(piece * k, piece * (k + 1)), x_last[:, k]) for k in range(2)]
        acts = [tail.tile([P, 2, 4, piece], F32, name="act", tag=f"act{b}") for b in range(2)]
        d_last = tail.tile([P, 2, 2, 4 * piece], BF16, name="d_last", tag="old_lower", align_bytes=64)
        d_pieces = []
        for k in range(2):
            for b in range(2):
                gelu_half(b, acts[b][:, k], *x_pieces[k])
                weave_on_vector(b, acts[b][:, k], d_last[:, k])
            d_pieces.append(quantize_d(d_last[:, k]))
        for k, copy in enumerate((nc.scalar.copy, nc.vector.tensor_copy)):
            c0 = GROUP + piece * k
            finish(j0 + piece * k, results[:, :, c0 : c0 + piece], *d_pieces[k], copy)
